import numpy as np
import ml_dtypes


def mxq(x, axis, fmt="e4m3"):
    dtype, down = {"e4m3": (ml_dtypes.float8_e4m3fn, 7), "e5m2": (ml_dtypes.float8_e5m2, 14)}[fmt]
    v = np.moveaxis(np.asarray(x, np.float32).astype(ml_dtypes.bfloat16).astype(np.float64), axis, -1)
    blocks = v.reshape(v.shape[:-1] + (-1, 32))
    amax = np.abs(blocks).max(-1, keepdims=True)
    byte = np.maximum(np.where(amax > 0, np.frexp(amax)[1] - 1 + 127, 0) - down, 1)
    scale = np.exp2(byte - 127.0)
    codes = (blocks / scale).astype(np.float32).astype(dtype).astype(np.float64)
    return np.moveaxis((codes * scale).reshape(v.shape), -1, axis)


WIDE = False


def mx_kscale(k):
    if not WIDE:
        return np.ones(k)
    levels = np.array([24, -24, 12, -12, 0])
    if k % 512:
        return np.exp2(np.random.permutation(np.resize(levels, k // 32))).repeat(32)
    a = np.empty((k // 512, 16))
    for p in range(k // 512):
        a[p, :8] = np.random.permutation(np.resize(levels, 8))
        for g in range(8):
            far = levels[np.abs(levels - a[p, g]) >= 10]
            a[p, g + 8] = far[np.random.randint(len(far))]
    return np.exp2(a.ravel()).repeat(32)


def f64(x):
    return np.asarray(x).astype(np.float64)


def striped(idx):
    return np.tile(idx.reshape(-1, 16).T, (8, 1)).astype(np.uint16)


def unstriped(offs):
    return offs[:16].T.reshape(-1).astype(np.int64)


E2M1 = np.array([0.0, 0.5, 1.0, 1.5, 2.0, 3.0, 4.0, 6.0, -0.0, -0.5, -1.0, -1.5, -2.0, -3.0, -4.0, -6.0])


def pack_weight(w, fmt):
    k, n = w.shape
    w = f64(np.asarray(w, np.float32).astype(ml_dtypes.bfloat16)).reshape(k // 32, 32, n)
    amax = np.abs(w).max(1)
    if fmt == "e4m3":
        byte = np.frexp(amax)[1] - 1 + 127 - 7
    else:
        mant, ex = np.frexp(amax / 6.0)
        byte = np.where(mant > 0.5, ex, ex - 1) + 127
    byte = np.clip(np.where(amax > 0, byte, 1), 1, 254)
    scaled = (w * np.exp2(127.0 - byte)[:, None, :]).reshape(k, n).astype(np.float32)
    by_word = np.ascontiguousarray(scaled.reshape(k // 512, 128, 4, n).transpose(0, 1, 3, 2))
    if fmt == "e4m3":
        words = by_word.astype(ml_dtypes.float8_e4m3fn).view(np.uint8)
    else:
        c = by_word.astype(ml_dtypes.float4_e2m1fn).view(np.uint8) & 0xF
        words = (c[..., 0::2] | (c[..., 1::2] << 4)).reshape(k // 512, 128, 2 * n)
    return np.ascontiguousarray(words), np.ascontiguousarray(byte.astype(np.uint8).reshape(k // 512, 16, n))


def unpack_weight(words, scales, fmt):
    g, _, n = scales.shape
    words = np.ascontiguousarray(words).reshape(g, 128, n, -1)
    if fmt == "e4m3":
        vals = words.view(ml_dtypes.float8_e4m3fn).astype(np.float64)
    else:
        nib = np.empty((g, 128, n, 4), np.uint8)
        nib[..., 0::2] = words & 0xF
        nib[..., 1::2] = words >> 4
        vals = E2M1[nib]
    vals = vals * np.repeat(np.exp2(scales.astype(np.float64) - 127.0), 8, axis=1)[..., None]
    return vals.transpose(0, 1, 3, 2).reshape(g * 512, n)


def silu(f):
    return f / (1.0 + np.exp(-np.maximum(f, -700.0)))


K, N, T, J = 1536, 512, 2048, 1024


def setup_inputs():
    n = np.random.standard_normal
    s = mx_kscale(K)[:, None]
    p_tab = pack_weight(n((K, T)) * s, "e4m3")
    p_wk = pack_weight(n((K, N)) / np.sqrt(K) / s, "e4m3")
    return {
        "tab_words": p_tab[0],
        "tab_scales": p_tab[1],
        "wk_words": p_wk[0],
        "wk_scales": p_wk[1],
        "wv": (n((K, N)) / np.sqrt(K) / s).astype(np.float32),
        "st": (n((N, J))).astype(np.float32),
        "res": (n((N, J))).astype(np.float32),
        "offs": striped(np.random.permutation(T)[:J]),
    }


def reference(tab_words, tab_scales, wk_words, wk_scales, wv, st, res, offs):
    idx = unstriped(offs)
    tab_ = unpack_weight(tab_words, tab_scales, "e4m3")[:, idx]
    wk_ = unpack_weight(wk_words, wk_scales, "e4m3")
    wv_ = mxq(f64(wv), 0, "e4m3")
    ke = wk_.T @ tab_
    ve = wv_.T @ tab_
    gate = silu(ke * f64(st))
    return f64(res) + gate * ve

@@ -1,0 +1,206 @@
+from contextlib import ExitStack
+
+import concourse.mybir as mybir
+
+K, N, T, J = 1536, 512, 2048, 1024
+FLOPS = 2 * 2 * K * N * J
+
+F32 = mybir.dt.float32
+BF16 = mybir.dt.bfloat16
+I32 = mybir.dt.int32
+U32 = mybir.dt.uint32
+U16 = mybir.dt.uint16
+U8 = mybir.dt.uint8
+FP8X4 = mybir.dt.float8_e4m3fn_x4
+MULT = mybir.AluOpType.mult
+ADD = mybir.AluOpType.add
+SILU = mybir.ActivationFunctionType.Silu
+
+P = 128
+PACK = 4
+PASSES = K // (P * PACK)
+QUADS = 4
+BANK = 512
+HALVES = J // BANK
+NT = N // P
+CHUNKS = NT * HALVES
+POOL_CHUNKS = 5
+
+
+def tile_list_engram_silu_kernel(tc, tab_words, tab_scales, wk_words, wk_scales, wv, st, res, offs, out):
+    nc = tc.nc
+    with ExitStack() as ctx:
+        keep = ctx.enter_context(tc.tile_pool(name="keep", bufs=1))
+        ke_psum = ctx.enter_context(tc.psum_pool(name="ke_psum", bufs=4))
+        ve_psum = ctx.enter_context(tc.psum_pool(name="ve_psum", bufs=4))
+
+        def sb(name, shape, dtype):
+            return keep.tile(shape, dtype, name=name, align_bytes=64)
+
+        offsets = sb("offsets", [P, J // 16], U16)
+        tab = [sb(f"tab{a}", [P, T], I32) for a in range(PASSES)]
+        tab_sc = sb("tab_sc", [P, T // 4], I32)
+        wk = sb("wk", [P, PASSES, N], I32)
+        wk_sc = sb("wk_sc", [P, PASSES, N // 4], I32)
+        wv_raw = [sb(f"wv_raw{a}", [P, PACK, N], F32) for a in range(PASSES)]
+        wv_bf = [sb(f"wv_bf{a}", [P, N, PACK], BF16) for a in range(PASSES)]
+        wv_q = [sb(f"wv_q{a}", [P, N], U32) for a in range(PASSES)]
+        wv_sc = [sb(f"wv_sc{a}", [P, N], U8) for a in range(PASSES)]
+        got = [sb(f"got{a}", [P, J], U32) for a in range(PASSES)]
+        got_sc = sb("got_sc", [P, J], U8)
+        st_sb = [sb(f"st{n}", [P, J], F32) for n in range(NT)]
+        res_sb = [sb(f"res{n}", [P, J], F32) for n in range(NT)]
+        zero = sb("zero", [P, 1], F32)
+        bias0 = sb("bias0", [P, 1], F32)
+
+        nc.vector.memset(tab_sc[:], 0)
+        nc.vector.memset(wk_sc[:], 0)
+        nc.vector.memset(zero[:], 0.0)
+        nc.scalar.activation(out=bias0[:], in_=zero[:], func=SILU)
+
+        def load_tab(a):
+            nc.sync.dma_start(out=tab[a][:], in_=tab_words[a].rearrange("p t i -> p (t i)").bitcast(I32))
+
+        def load_wv(a):
+            rows = wv[a * P * PACK : (a + 1) * P * PACK, :]
+            nc.sync.dma_start(out=wv_raw[a][:], in_=rows.rearrange("(p i) n -> p i n", i=PACK))
+
+        def load_rows(tiles, src, n):
+            nc.sync.dma_start(out=tiles[n][:], in_=src[n * P : (n + 1) * P, :])
+
+        for q in range(QUADS):
+            nc.scalar.dma_start(
+                out=tab_sc[32 * q : 32 * q + 4 * PASSES, :],
+                in_=tab_scales[:, 4 * q : 4 * q + 4, :].bitcast(I32),
+            )
+        nc.sync.dma_start(offsets[:], offs)
+        load_tab(0)
+        for q in range(QUADS):
+            nc.sync.dma_start(
+                out=wk_sc[32 * q : 32 * q + 4, :, :],
+                in_=wk_scales[:, 4 * q : 4 * q + 4, :].rearrange("a r n -> r a n").bitcast(I32),
+            )
+        nc.sync.dma_start(out=wk[:], in_=wk_words.rearrange("a p n i -> p a (n i)").bitcast(I32))
+        load_tab(1)
+        load_tab(2)
+        load_wv(0)
+        load_rows(st_sb, st, 0)
+        load_wv(1)
+        load_wv(2)
+        load_rows(st_sb, st, 1)
+        load_rows(res_sb, res, 0)
+        load_rows(st_sb, st, 2)
+        load_rows(res_sb, res, 1)
+        load_rows(st_sb, st, 3)
+        load_rows(res_sb, res, 2)
+        load_rows(res_sb, res, 3)
+
+        def gather_words(a, j0, j1):
+            window = tab[a][:].bitcast(U32)
+            nc.vector.tensor_copy(out=got[a][:, j0:j1], in_=window.indirect(offsets[:, j0 // 16 : j1 // 16]))
+
+        def cast(copy, a, n0, n1):
+            copy(
+                out=wv_bf[a][:, n0:n1, :].rearrange("p (c u) i -> p c i u", u=4),
+                in_=wv_raw[a][:, :, n0:n1].rearrange("p i (c u) -> p c i u", u=4),
+            )
+
+        def quantize(a, n0, n1):
+            nc.vector.quantize_mx(
+                out=wv_q[a][:, n0:n1].bitcast(FP8X4),
+                scales=wv_sc[a][:, n0:n1],
+                in_=wv_bf[a][:, n0:n1, :].rearrange("p n i -> p (n i)"),
+            )
+
+        def ncols(c):
+            return slice((c // HALVES) * P, (c // HALVES + 1) * P)
+
+        def jcols(c):
+            return slice((c % HALVES) * BANK, (c % HALVES + 1) * BANK)
+
+        def mx_pass(acc, c, a, words, scales):
+            nc.tensor.matmul_mx(
+                out=acc[:],
+                lhsT=words.bitcast(FP8X4),
+                lhsT_scale=scales,
+                rhs=got[a][:, jcols(c)].bitcast(FP8X4),
+                rhs_scale=got_sc[4 * a : P, jcols(c)],
+                start=(a == 0),
+                stop=(a == PASSES - 1),
+            )
+
+        ke, ve, gate, prod = {}, {}, {}, {}
+
+        def ke_pass(c, a):
+            if a == 0:
+                ke[c] = ke_psum.tile([P, BANK], F32, name="ke")
+            mx_pass(ke[c], c, a, wk[:, a, ncols(c)], wk_sc[:].bitcast(U8)[:, a, ncols(c)])
+
+        def ve_pass(c, a):
+            if a == 0:
+                ve[c] = ve_psum.tile([P, BANK], F32, name="ve")
+            mx_pass(ve[c], c, a, wv_q[a][:, ncols(c)], wv_sc[a][:, ncols(c)])
+
+        def make_gate(c):
+            s = sb(f"s{c}", [P, BANK], F32)
+            nc.vector.tensor_tensor(out=s[:], in0=ke[c][:], in1=st_sb[c // HALVES][:, jcols(c)], op=MULT)
+            gate[c] = sb(f"gate{c}", [P, BANK], F32)
+            nc.scalar.activation(out=gate[c][:], in_=s[:], func=SILU, bias=bias0[:])
+
+        def gate_value(c):
+            prod[c] = sb(f"prod{c}", [P, BANK], F32)
+            nc.vector.tensor_tensor(out=prod[c][:], in0=ve[c][:], in1=gate[c][:], op=MULT)
+
+        def finish(c):
+            o = sb(f"o{c}", [P, BANK], F32)
+            eng = nc.gpsimd if c < POOL_CHUNKS else nc.vector
+            eng.tensor_tensor(out=o[:], in0=prod[c][:], in1=res_sb[c // HALVES][:, jcols(c)], op=ADD)
+            nc.sync.dma_start(out=out[ncols(c), jcols(c)], in_=o[:])
+
+        first = range(4)
+        gather_words(0, 0, J)
+        nc.vector.tensor_copy(out=got_sc[:], in_=tab_sc[:].bitcast(U8).indirect(offsets[:]))
+        for c in first:
+            ke_pass(c, 0)
+        gather_words(1, 0, J)
+        for c in first:
+            ke_pass(c, 1)
+        gather_words(2, 0, BANK)
+        gather_words(2, BANK, J)
+        for c in (0, 2, 1, 3):
+            ke_pass(c, 2)
+        cast(nc.scalar.copy, 0, 0, N)
+        make_gate(0)
+        make_gate(1)
+        quantize(0, 0, N)
+        for a in range(PASSES):
+            ke_pass(4, a)
+        for c in first:
+            ve_pass(c, 0)
+        cast(nc.vector.tensor_copy, 1, 0, N)
+        for a in range(PASSES):
+            ke_pass(5, a)
+        quantize(1, 0, N)
+        for c in first:
+            ve_pass(c, 1)
+        cast(nc.vector.tensor_copy, 2, 0, N // 2)
+        cast(nc.scalar.copy, 2, N // 2, N)
+        quantize(2, 0, N // 2)
+        for c in first:
+            ve_pass(c, 2)
+        make_gate(2)
+        quantize(2, N // 2, N)
+        for c in range(CHUNKS):
+            gate_value(c)
+            if c + 6 < CHUNKS:
+                for a in range(PASSES):
+                    ke_pass(c + 6, a)
+            if c + 4 < CHUNKS:
+                for a in range(PASSES):
+                    ve_pass(c + 4, a)
+            if c + 3 < CHUNKS:
+                make_gate(c + 3)
+            if c < POOL_CHUNKS:
+                finish(c)
+        for c in range(POOL_CHUNKS, CHUNKS):
+            finish(c)

@@ -25,14 +25,15 @@ HALVES = J // BANK
 NT = N // P
 CHUNKS = NT * HALVES
 POOL_CHUNKS = 5
+BANKS = 8
+KE_FIRST = 6
 
 
 def tile_list_engram_silu_kernel(tc, tab_words, tab_scales, wk_words, wk_scales, wv, st, res, offs, out):
     nc = tc.nc
     with ExitStack() as ctx:
         keep = ctx.enter_context(tc.tile_pool(name="keep", bufs=1))
-        ke_psum = ctx.enter_context(tc.psum_pool(name="ke_psum", bufs=4))
-        ve_psum = ctx.enter_context(tc.psum_pool(name="ve_psum", bufs=4))
+        psum = ctx.enter_context(tc.psum_pool(name="psum", bufs=1))
 
         def sb(name, shape, dtype):
             return keep.tile(shape, dtype, name=name, align_bytes=64)
@@ -50,13 +51,13 @@ def tile_list_engram_silu_kernel(tc, tab_words, tab_scales, wk_words, wk_scales,
         got_sc = sb("got_sc", [P, J], U8)
         st_sb = [sb(f"st{n}", [P, J], F32) for n in range(NT)]
         res_sb = [sb(f"res{n}", [P, J], F32) for n in range(NT)]
+        out_sb = [sb(f"out{n}", [P, J], F32) for n in range(NT)]
         zero = sb("zero", [P, 1], F32)
         bias0 = sb("bias0", [P, 1], F32)
 
         nc.vector.memset(tab_sc[:], 0)
         nc.vector.memset(wk_sc[:], 0)
         nc.vector.memset(zero[:], 0.0)
-        nc.scalar.activation(out=bias0[:], in_=zero[:], func=SILU)
 
         def load_tab(a):
             nc.sync.dma_start(out=tab[a][:], in_=tab_words[a].rearrange("p t i -> p (t i)").bitcast(I32))
@@ -65,30 +66,37 @@ def tile_list_engram_silu_kernel(tc, tab_words, tab_scales, wk_words, wk_scales,
             rows = wv[a * P * PACK : (a + 1) * P * PACK, :]
             nc.sync.dma_start(out=wv_raw[a][:], in_=rows.rearrange("(p i) n -> p i n", i=PACK))
 
-        def load_rows(tiles, src, n):
-            nc.sync.dma_start(out=tiles[n][:], in_=src[n * P : (n + 1) * P, :])
+        def load_rows(tiles, src, n, j0=0, j1=J):
+            nc.sync.dma_start(out=tiles[n][:, j0:j1], in_=src[n * P : (n + 1) * P, j0:j1])
 
+        def load_wk(a0, a1):
+            nc.sync.dma_start(out=wk[:, a0:a1, :], in_=wk_words[a0:a1].rearrange("a p n i -> p a (n i)").bitcast(I32))
+
+        load_tab(0)
+        nc.sync.dma_start(offsets[:], offs)
         for q in range(QUADS):
-            nc.scalar.dma_start(
+            queue = nc.sync if q < QUADS // 2 else nc.scalar
+            queue.dma_start(
                 out=tab_sc[32 * q : 32 * q + 4 * PASSES, :],
                 in_=tab_scales[:, 4 * q : 4 * q + 4, :].bitcast(I32),
             )
-        nc.sync.dma_start(offsets[:], offs)
-        load_tab(0)
+        nc.scalar.activation(out=bias0[:], in_=zero[:], func=SILU)
+        load_tab(1)
+        load_wk(0, PASSES)
         for q in range(QUADS):
             nc.sync.dma_start(
                 out=wk_sc[32 * q : 32 * q + 4, :, :],
                 in_=wk_scales[:, 4 * q : 4 * q + 4, :].rearrange("a r n -> r a n").bitcast(I32),
             )
-        nc.sync.dma_start(out=wk[:], in_=wk_words.rearrange("a p n i -> p a (n i)").bitcast(I32))
-        load_tab(1)
         load_tab(2)
         load_wv(0)
-        load_rows(st_sb, st, 0)
         load_wv(1)
         load_wv(2)
+        load_rows(st_sb, st, 0, 0, BANK)
+        load_rows(st_sb, st, 0, BANK, J)
+        load_rows(res_sb, res, 0, 0, BANK)
         load_rows(st_sb, st, 1)
-        load_rows(res_sb, res, 0)
+        load_rows(res_sb, res, 0, BANK, J)
         load_rows(st_sb, st, 2)
         load_rows(res_sb, res, 1)
         load_rows(st_sb, st, 3)
@@ -130,77 +138,94 @@ def tile_list_engram_silu_kernel(tc, tab_words, tab_scales, wk_words, wk_scales,
             )
 
         ke, ve, gate, prod = {}, {}, {}, {}
+        free_banks = list(range(BANKS))
+        bank_of = {}
+
+        def take_bank(key):
+            bank_of[key] = free_banks.pop(0)
+            return psum.tile([P, BANK], F32, name=f"bank{bank_of[key]}")
 
         def ke_pass(c, a):
             if a == 0:
-                ke[c] = ke_psum.tile([P, BANK], F32, name="ke")
+                ke[c] = take_bank(("ke", c))
             mx_pass(ke[c], c, a, wk[:, a, ncols(c)], wk_sc[:].bitcast(U8)[:, a, ncols(c)])
 
         def ve_pass(c, a):
             if a == 0:
-                ve[c] = ve_psum.tile([P, BANK], F32, name="ve")
+                ve[c] = take_bank(("ve", c))
             mx_pass(ve[c], c, a, wv_q[a][:, ncols(c)], wv_sc[a][:, ncols(c)])
 
         def make_gate(c):
             s = sb(f"s{c}", [P, BANK], F32)
             nc.vector.tensor_tensor(out=s[:], in0=ke[c][:], in1=st_sb[c // HALVES][:, jcols(c)], op=MULT)
+            free_banks.append(bank_of[("ke", c)])
             gate[c] = sb(f"gate{c}", [P, BANK], F32)
             nc.scalar.activation(out=gate[c][:], in_=s[:], func=SILU, bias=bias0[:])
 
         def gate_value(c):
             prod[c] = sb(f"prod{c}", [P, BANK], F32)
             nc.vector.tensor_tensor(out=prod[c][:], in0=ve[c][:], in1=gate[c][:], op=MULT)
+            free_banks.append(bank_of[("ve", c)])
 
-        def finish(c):
-            o = sb(f"o{c}", [P, BANK], F32)
-            eng = nc.gpsimd if c < POOL_CHUNKS else nc.vector
-            eng.tensor_tensor(out=o[:], in0=prod[c][:], in1=res_sb[c // HALVES][:, jcols(c)], op=ADD)
-            nc.sync.dma_start(out=out[ncols(c), jcols(c)], in_=o[:])
+        def add(eng, c, j0, j1):
+            n, base = c // HALVES, (c % HALVES) * BANK
+            cols = slice(base + j0, base + j1)
+            eng.tensor_tensor(out=out_sb[n][:, cols], in0=prod[c][:, j0:j1], in1=res_sb[n][:, cols], op=ADD)
 
-        first = range(4)
+        def store(c):
+            n = c // HALVES
+            if n >= NT // 2:
+                nc.sync.dma_start(out=out[ncols(c), jcols(c)], in_=out_sb[n][:, jcols(c)])
+            elif c % HALVES == HALVES - 1:
+                nc.sync.dma_start(out=out[ncols(c), :], in_=out_sb[n][:])
+
+        ke_first = range(KE_FIRST)
+        ve_first = range(BANKS - KE_FIRST)
         gather_words(0, 0, J)
         nc.vector.tensor_copy(out=got_sc[:], in_=tab_sc[:].bitcast(U8).indirect(offsets[:]))
-        for c in first:
-            ke_pass(c, 0)
         gather_words(1, 0, J)
-        for c in first:
-            ke_pass(c, 1)
-        gather_words(2, 0, BANK)
-        gather_words(2, BANK, J)
-        for c in (0, 2, 1, 3):
-            ke_pass(c, 2)
+        gather_words(2, 0, J)
+        for a in range(PASSES):
+            for c in ke_first:
+                ke_pass(c, a)
         cast(nc.scalar.copy, 0, 0, N)
-        make_gate(0)
-        make_gate(1)
-        quantize(0, 0, N)
-        for a in range(PASSES):
-            ke_pass(4, a)
-        for c in first:
-            ve_pass(c, 0)
-        cast(nc.vector.tensor_copy, 1, 0, N)
-        for a in range(PASSES):
-            ke_pass(5, a)
-        quantize(1, 0, N)
-        for c in first:
-            ve_pass(c, 1)
-        cast(nc.vector.tensor_copy, 2, 0, N // 2)
-        cast(nc.scalar.copy, 2, N // 2, N)
+        cast(nc.vector.tensor_copy, 1, 0, N // 2)
+        cast(nc.scalar.copy, 1, N // 2, N)
+        for a in range(2):
+            quantize(a, 0, N)
+            for c in ve_first:
+                ve_pass(c, a)
+        cast(nc.vector.tensor_copy, 2, 0, P)
+        cast(nc.scalar.copy, 2, P, 2 * P)
+        cast(nc.scalar.copy, 2, 2 * P, N)
         quantize(2, 0, N // 2)
-        for c in first:
+        for c in ve_first:
             ve_pass(c, 2)
-        make_gate(2)
-        quantize(2, N // 2, N)
+
+        steps = [("ke", 0)]
         for c in range(CHUNKS):
-            gate_value(c)
-            if c + 6 < CHUNKS:
+            if c + 1 < CHUNKS:
+                steps.append(("ke", c + 1))
+            steps.append(("ve", c))
+        later = [key for key in steps if key not in bank_of]
+
+        for kind, c in steps:
+            if kind == "ke":
+                make_gate(c)
+            else:
+                if c == 0:
+                    quantize(2, N // 2, N)
+                gate_value(c)
+            if later:
+                next_kind, next_c = later.pop(0)
                 for a in range(PASSES):
-                    ke_pass(c + 6, a)
-            if c + 4 < CHUNKS:
-                for a in range(PASSES):
-                    ve_pass(c + 4, a)
-            if c + 3 < CHUNKS:
-                make_gate(c + 3)
-            if c < POOL_CHUNKS:
-                finish(c)
+                    (ke_pass if next_kind == "ke" else ve_pass)(next_c, a)
+            if kind == "ve":
+                if c < POOL_CHUNKS:
+                    add(nc.gpsimd, c, 0, BANK)
+                    store(c)
+                elif c == POOL_CHUNKS:
+                    add(nc.gpsimd, c, 0, BANK // 2)
         for c in range(POOL_CHUNKS, CHUNKS):
-            finish(c)
+            add(nc.vector, c, BANK // 2 if c == POOL_CHUNKS else 0, BANK)
+            store(c)

@@ -21,12 +21,13 @@ PACK = 4
 PASSES = K // (P * PACK)
 QUADS = 4
 BANK = 512
+BANKS = 8
 HALVES = J // BANK
 NT = N // P
 CHUNKS = NT * HALVES
 POOL_CHUNKS = 5
-BANKS = 8
 KE_FIRST = 6
+WHOLE_STORES = 2
 
 
 def tile_list_engram_silu_kernel(tc, tab_words, tab_scales, wk_words, wk_scales, wv, st, res, offs, out):
@@ -35,77 +36,92 @@ def tile_list_engram_silu_kernel(tc, tab_words, tab_scales, wk_words, wk_scales,
         keep = ctx.enter_context(tc.tile_pool(name="keep", bufs=1))
         psum = ctx.enter_context(tc.psum_pool(name="psum", bufs=1))
 
-        def sb(name, shape, dtype):
-            return keep.tile(shape, dtype, name=name, align_bytes=64)
+        def sb(name, shape, dtype, tag=None):
+            return keep.tile(shape, dtype, name=name, tag=tag or name, align_bytes=64)
 
         offsets = sb("offsets", [P, J // 16], U16)
-        tab = [sb(f"tab{a}", [P, T], I32) for a in range(PASSES)]
         tab_sc = sb("tab_sc", [P, T // 4], I32)
         wk = sb("wk", [P, PASSES, N], I32)
         wk_sc = sb("wk_sc", [P, PASSES, N // 4], I32)
-        wv_raw = [sb(f"wv_raw{a}", [P, PACK, N], F32) for a in range(PASSES)]
         wv_bf = [sb(f"wv_bf{a}", [P, N, PACK], BF16) for a in range(PASSES)]
         wv_q = [sb(f"wv_q{a}", [P, N], U32) for a in range(PASSES)]
         wv_sc = [sb(f"wv_sc{a}", [P, N], U8) for a in range(PASSES)]
         got = [sb(f"got{a}", [P, J], U32) for a in range(PASSES)]
         got_sc = sb("got_sc", [P, J], U8)
-        st_sb = [sb(f"st{n}", [P, J], F32) for n in range(NT)]
-        res_sb = [sb(f"res{n}", [P, J], F32) for n in range(NT)]
-        out_sb = [sb(f"out{n}", [P, J], F32) for n in range(NT)]
+        out_sb = [sb(f"out{n}", [P, J], F32) for n in range(NT - 1)]
         zero = sb("zero", [P, 1], F32)
         bias0 = sb("bias0", [P, 1], F32)
+        tab, wv_raw, st_sb, res_sb = {}, {}, {}, {}
 
         nc.vector.memset(tab_sc[:], 0)
         nc.vector.memset(wk_sc[:], 0)
         nc.vector.memset(zero[:], 0.0)
 
-        def load_tab(a):
-            nc.sync.dma_start(out=tab[a][:], in_=tab_words[a].rearrange("p t i -> p (t i)").bitcast(I32))
+        def load_tab(a0, a1, queue=nc.sync):
+            tile = sb(f"tab{a0}", [P, a1 - a0, T], I32)
+            queue.dma_start(out=tile[:], in_=tab_words[a0:a1].rearrange("a p t i -> p a (t i)").bitcast(I32))
+            for a in range(a0, a1):
+                tab[a] = tile[:, a - a0, :]
 
-        def load_wv(a):
-            rows = wv[a * P * PACK : (a + 1) * P * PACK, :]
-            nc.sync.dma_start(out=wv_raw[a][:], in_=rows.rearrange("(p i) n -> p i n", i=PACK))
+        def load_wv(a0, a1, queue=nc.sync):
+            tile = sb(f"wv_raw{a0}", [P, a1 - a0, PACK * N], F32)
+            rows = wv[a0 * P * PACK : a1 * P * PACK, :]
+            queue.dma_start(out=tile[:], in_=rows.rearrange("(a p i) n -> p a (i n)", p=P, i=PACK))
+            for a in range(a0, a1):
+                wv_raw[a] = tile[:, a - a0, :].rearrange("p (i n) -> p i n", i=PACK)
 
-        def load_rows(tiles, src, n, j0=0, j1=J):
-            nc.sync.dma_start(out=tiles[n][:, j0:j1], in_=src[n * P : (n + 1) * P, j0:j1])
+        def load_rows(name, tiles, src, n0, n1, queue=nc.sync):
+            tile = sb(f"{name}{n0}", [P, n1 - n0, J], F32)
+            queue.dma_start(out=tile[:], in_=src[n0 * P : n1 * P, :].rearrange("(c p) j -> p c j", p=P))
+            for n in range(n0, n1):
+                tiles[n] = tile[:, n - n0, :]
 
-        def load_wk(a0, a1):
-            nc.sync.dma_start(out=wk[:, a0:a1, :], in_=wk_words[a0:a1].rearrange("a p n i -> p a (n i)").bitcast(I32))
+        def load_half(name, tiles, src, n, h):
+            if h == 0:
+                tiles[n] = sb(f"{name}{n}", [P, J], F32)[:]
+            nc.sync.dma_start(out=tiles[n][:, h * BANK : (h + 1) * BANK], in_=src[n * P : (n + 1) * P, h * BANK : (h + 1) * BANK])
 
-        load_tab(0)
-        nc.sync.dma_start(offsets[:], offs)
-        for q in range(QUADS):
-            queue = nc.sync if q < QUADS // 2 else nc.scalar
+        def load_wk(a0, a1, queue=nc.sync):
+            queue.dma_start(out=wk[:, a0:a1, :], in_=wk_words[a0:a1].rearrange("a p n i -> p a (n i)").bitcast(I32))
+
+        def load_tab_scales(q, queue):
             queue.dma_start(
                 out=tab_sc[32 * q : 32 * q + 4 * PASSES, :],
                 in_=tab_scales[:, 4 * q : 4 * q + 4, :].bitcast(I32),
             )
-        nc.scalar.activation(out=bias0[:], in_=zero[:], func=SILU)
-        load_tab(1)
-        load_wk(0, PASSES)
-        for q in range(QUADS):
-            nc.sync.dma_start(
+
+        def load_wk_scales(q, queue=nc.sync):
+            queue.dma_start(
                 out=wk_sc[32 * q : 32 * q + 4, :, :],
                 in_=wk_scales[:, 4 * q : 4 * q + 4, :].rearrange("a r n -> r a n").bitcast(I32),
             )
-        load_tab(2)
-        load_wv(0)
-        load_wv(1)
-        load_wv(2)
-        load_rows(st_sb, st, 0, 0, BANK)
-        load_rows(st_sb, st, 0, BANK, J)
-        load_rows(res_sb, res, 0, 0, BANK)
-        load_rows(st_sb, st, 1)
-        load_rows(res_sb, res, 0, BANK, J)
-        load_rows(st_sb, st, 2)
-        load_rows(res_sb, res, 1)
-        load_rows(st_sb, st, 3)
-        load_rows(res_sb, res, 2)
-        load_rows(res_sb, res, 3)
 
-        def gather_words(a, j0, j1):
-            window = tab[a][:].bitcast(U32)
-            nc.vector.tensor_copy(out=got[a][:, j0:j1], in_=window.indirect(offsets[:, j0 // 16 : j1 // 16]))
+        load_tab(0, 1)
+        nc.sync.dma_start(offsets[:], offs)
+        for q in range(QUADS):
+            load_tab_scales(q, nc.sync if q < QUADS // 2 else nc.scalar)
+        nc.scalar.activation(out=bias0[:], in_=zero[:], func=SILU)
+        load_tab(1, 2)
+        load_wk(0, 3)
+        for q in range(QUADS):
+            load_wk_scales(q)
+        load_tab(2, 3)
+        load_wv(0, 1)
+        load_wv(1, 2)
+        load_wv(2, 3)
+        load_half("st", st_sb, st, 0, 0)
+        load_half("st", st_sb, st, 0, 1)
+        load_half("res", res_sb, res, 0, 0)
+        load_rows("st", st_sb, st, 1, 2)
+        load_half("res", res_sb, res, 0, 1)
+        load_rows("st", st_sb, st, 2, 3)
+        load_rows("res", res_sb, res, 1, 2)
+        load_rows("st", st_sb, st, 3, 4)
+        load_rows("res", res_sb, res, 2, 3)
+        load_rows("res", res_sb, res, 3, 4)
+
+        def gather_words(a):
+            nc.vector.tensor_copy(out=got[a][:], in_=tab[a].bitcast(U32).indirect(offsets[:]))
 
         def cast(copy, a, n0, n1):
             copy(
@@ -126,9 +142,19 @@ def tile_list_engram_silu_kernel(tc, tab_words, tab_scales, wk_words, wk_scales,
         def jcols(c):
             return slice((c % HALVES) * BANK, (c % HALVES + 1) * BANK)
 
-        def mx_pass(acc, c, a, words, scales):
+        free_banks = list(range(BANKS))
+        bank_of, acc, gate, prod = {}, {}, {}, {}
+
+        def mx_pass(kind, c, a):
+            if a == 0:
+                bank_of[kind, c] = free_banks.pop(0)
+                acc[kind, c] = psum.tile([P, BANK], F32, name=f"bank{bank_of[kind, c]}")
+            if kind == "ke":
+                words, scales = wk[:, a, ncols(c)], wk_sc[:].bitcast(U8)[:, a, ncols(c)]
+            else:
+                words, scales = wv_q[a][:, ncols(c)], wv_sc[a][:, ncols(c)]
             nc.tensor.matmul_mx(
-                out=acc[:],
+                out=acc[kind, c][:],
                 lhsT=words.bitcast(FP8X4),
                 lhsT_scale=scales,
                 rhs=got[a][:, jcols(c)].bitcast(FP8X4),
@@ -137,77 +163,54 @@ def tile_list_engram_silu_kernel(tc, tab_words, tab_scales, wk_words, wk_scales,
                 stop=(a == PASSES - 1),
             )
 
-        ke, ve, gate, prod = {}, {}, {}, {}
-        free_banks = list(range(BANKS))
-        bank_of = {}
-
-        def take_bank(key):
-            bank_of[key] = free_banks.pop(0)
-            return psum.tile([P, BANK], F32, name=f"bank{bank_of[key]}")
-
-        def ke_pass(c, a):
-            if a == 0:
-                ke[c] = take_bank(("ke", c))
-            mx_pass(ke[c], c, a, wk[:, a, ncols(c)], wk_sc[:].bitcast(U8)[:, a, ncols(c)])
-
-        def ve_pass(c, a):
-            if a == 0:
-                ve[c] = take_bank(("ve", c))
-            mx_pass(ve[c], c, a, wv_q[a][:, ncols(c)], wv_sc[a][:, ncols(c)])
-
         def make_gate(c):
-            s = sb(f"s{c}", [P, BANK], F32)
-            nc.vector.tensor_tensor(out=s[:], in0=ke[c][:], in1=st_sb[c // HALVES][:, jcols(c)], op=MULT)
-            free_banks.append(bank_of[("ke", c)])
+            s = sb(f"s{c}", [P, BANK], F32, tag="last" if c == CHUNKS - 1 else None)
+            nc.vector.tensor_tensor(out=s[:], in0=acc["ke", c][:], in1=st_sb[c // HALVES][:, jcols(c)], op=MULT)
             gate[c] = sb(f"gate{c}", [P, BANK], F32)
             nc.scalar.activation(out=gate[c][:], in_=s[:], func=SILU, bias=bias0[:])
 
         def gate_value(c):
             prod[c] = sb(f"prod{c}", [P, BANK], F32)
-            nc.vector.tensor_tensor(out=prod[c][:], in0=ve[c][:], in1=gate[c][:], op=MULT)
-            free_banks.append(bank_of[("ve", c)])
+            nc.vector.tensor_tensor(out=prod[c][:], in0=acc["ve", c][:], in1=gate[c][:], op=MULT)
 
-        def add(eng, c, j0, j1):
-            n, base = c // HALVES, (c % HALVES) * BANK
-            cols = slice(base + j0, base + j1)
-            eng.tensor_tensor(out=out_sb[n][:, cols], in0=prod[c][:, j0:j1], in1=res_sb[n][:, cols], op=ADD)
-
-        def store(c):
+        def finish(c):
             n = c // HALVES
-            if n >= NT // 2:
+            nc.gpsimd.tensor_tensor(out=out_sb[n][:, jcols(c)], in0=prod[c][:], in1=res_sb[n][:, jcols(c)], op=ADD)
+            if n >= WHOLE_STORES:
                 nc.sync.dma_start(out=out[ncols(c), jcols(c)], in_=out_sb[n][:, jcols(c)])
             elif c % HALVES == HALVES - 1:
                 nc.sync.dma_start(out=out[ncols(c), :], in_=out_sb[n][:])
 
         ke_first = range(KE_FIRST)
         ve_first = range(BANKS - KE_FIRST)
-        gather_words(0, 0, J)
+        gather_words(0)
         nc.vector.tensor_copy(out=got_sc[:], in_=tab_sc[:].bitcast(U8).indirect(offsets[:]))
-        gather_words(1, 0, J)
-        gather_words(2, 0, J)
+        gather_words(1)
+        gather_words(2)
         for a in range(PASSES):
             for c in ke_first:
-                ke_pass(c, a)
+                mx_pass("ke", c, a)
         cast(nc.scalar.copy, 0, 0, N)
         cast(nc.vector.tensor_copy, 1, 0, N // 2)
         cast(nc.scalar.copy, 1, N // 2, N)
-        for a in range(2):
+        for a in range(PASSES - 1):
             quantize(a, 0, N)
+        for a in range(PASSES - 1):
             for c in ve_first:
-                ve_pass(c, a)
+                mx_pass("ve", c, a)
         cast(nc.vector.tensor_copy, 2, 0, P)
         cast(nc.scalar.copy, 2, P, 2 * P)
         cast(nc.scalar.copy, 2, 2 * P, N)
         quantize(2, 0, N // 2)
         for c in ve_first:
-            ve_pass(c, 2)
+            mx_pass("ve", c, 2)
 
         steps = [("ke", 0)]
         for c in range(CHUNKS):
             if c + 1 < CHUNKS:
                 steps.append(("ke", c + 1))
             steps.append(("ve", c))
-        later = [key for key in steps if key not in bank_of]
+        later = [step for step in steps if step not in bank_of]
 
         for kind, c in steps:
             if kind == "ke":
@@ -216,16 +219,15 @@ def tile_list_engram_silu_kernel(tc, tab_words, tab_scales, wk_words, wk_scales,
                 if c == 0:
                     quantize(2, N // 2, N)
                 gate_value(c)
+            free_banks.append(bank_of[kind, c])
             if later:
-                next_kind, next_c = later.pop(0)
+                step = later.pop(0)
                 for a in range(PASSES):
-                    (ke_pass if next_kind == "ke" else ve_pass)(next_c, a)
-            if kind == "ve":
-                if c < POOL_CHUNKS:
-                    add(nc.gpsimd, c, 0, BANK)
-                    store(c)
-                elif c == POOL_CHUNKS:
-                    add(nc.gpsimd, c, 0, BANK // 2)
+                    mx_pass(step[0], step[1], a)
+            if kind == "ve" and c < POOL_CHUNKS:
+                finish(c)
+        late = sb("late", [P, CHUNKS - POOL_CHUNKS, BANK], F32, tag="last")
         for c in range(POOL_CHUNKS, CHUNKS):
-            add(nc.vector, c, BANK // 2 if c == POOL_CHUNKS else 0, BANK)
-            store(c)
+            dst = late[:, c - POOL_CHUNKS, :]
+            nc.vector.tensor_tensor(out=dst, in0=prod[c][:], in1=res_sb[c // HALVES][:, jcols(c)], op=ADD)
+            nc.sync.dma_start(out=out[ncols(c), jcols(c)], in_=dst)

@@ -19,7 +19,9 @@ SILU = mybir.ActivationFunctionType.Silu
 P = 128
 PACK = 4
 PASSES = K // (P * PACK)
+LAST = PASSES - 1
 QUADS = 4
+SCALE_ROWS = 4
 BANK = 512
 BANKS = 8
 HALVES = J // BANK
@@ -39,6 +41,12 @@ def tile_list_engram_silu_kernel(tc, tab_words, tab_scales, wk_words, wk_scales,
         def sb(name, shape, dtype, tag=None):
             return keep.tile(shape, dtype, name=name, tag=tag or name, align_bytes=64)
 
+        def ncols(c):
+            return slice((c // HALVES) * P, (c // HALVES + 1) * P)
+
+        def jcols(c):
+            return slice((c % HALVES) * BANK, (c % HALVES + 1) * BANK)
+
         offsets = sb("offsets", [P, J // 16], U16)
         tab_sc = sb("tab_sc", [P, T // 4], I32)
         wk = sb("wk", [P, PASSES, N], I32)
@@ -48,82 +56,63 @@ def tile_list_engram_silu_kernel(tc, tab_words, tab_scales, wk_words, wk_scales,
         wv_sc = [sb(f"wv_sc{a}", [P, N], U8) for a in range(PASSES)]
         got = [sb(f"got{a}", [P, J], U32) for a in range(PASSES)]
         got_sc = sb("got_sc", [P, J], U8)
-        out_sb = [sb(f"out{n}", [P, J], F32) for n in range(NT - 1)]
         zero = sb("zero", [P, 1], F32)
-        bias0 = sb("bias0", [P, 1], F32)
+        silu_bias = sb("silu_bias", [P, 1], F32)
         tab, wv_raw, st_sb, res_sb = {}, {}, {}, {}
 
         nc.vector.memset(tab_sc[:], 0)
         nc.vector.memset(wk_sc[:], 0)
         nc.vector.memset(zero[:], 0.0)
 
-        def load_tab(a0, a1, queue=nc.sync):
+        def load_tab(a0, a1):
             tile = sb(f"tab{a0}", [P, a1 - a0, T], I32)
-            queue.dma_start(out=tile[:], in_=tab_words[a0:a1].rearrange("a p t i -> p a (t i)").bitcast(I32))
+            nc.sync.dma_start(out=tile[:], in_=tab_words[a0:a1].rearrange("a p t i -> p a (t i)").bitcast(I32))
             for a in range(a0, a1):
                 tab[a] = tile[:, a - a0, :]
 
-        def load_wv(a0, a1, queue=nc.sync):
-            tile = sb(f"wv_raw{a0}", [P, a1 - a0, PACK * N], F32)
-            rows = wv[a0 * P * PACK : a1 * P * PACK, :]
-            queue.dma_start(out=tile[:], in_=rows.rearrange("(a p i) n -> p a (i n)", p=P, i=PACK))
-            for a in range(a0, a1):
-                wv_raw[a] = tile[:, a - a0, :].rearrange("p (i n) -> p i n", i=PACK)
+        def load_wv(a):
+            wv_raw[a] = sb(f"wv_raw{a}", [P, PACK, N], F32)
+            rows = wv[a * P * PACK : (a + 1) * P * PACK, :]
+            nc.sync.dma_start(out=wv_raw[a][:], in_=rows.rearrange("(p i) n -> p i n", i=PACK))
 
-        def load_rows(name, tiles, src, n0, n1, queue=nc.sync):
+        def load_rows(name, tiles, src, n0, n1):
             tile = sb(f"{name}{n0}", [P, n1 - n0, J], F32)
-            queue.dma_start(out=tile[:], in_=src[n0 * P : n1 * P, :].rearrange("(c p) j -> p c j", p=P))
+            nc.sync.dma_start(out=tile[:], in_=src[n0 * P : n1 * P, :].rearrange("(c p) j -> p c j", p=P))
             for n in range(n0, n1):
                 tiles[n] = tile[:, n - n0, :]
-
-        def load_half(name, tiles, src, n, h):
-            if h == 0:
-                tiles[n] = sb(f"{name}{n}", [P, J], F32)[:]
-            nc.sync.dma_start(out=tiles[n][:, h * BANK : (h + 1) * BANK], in_=src[n * P : (n + 1) * P, h * BANK : (h + 1) * BANK])
-
-        def load_wk(a0, a1, queue=nc.sync):
-            queue.dma_start(out=wk[:, a0:a1, :], in_=wk_words[a0:a1].rearrange("a p n i -> p a (n i)").bitcast(I32))
-
-        def load_tab_scales(q, queue):
-            queue.dma_start(
-                out=tab_sc[32 * q : 32 * q + 4 * PASSES, :],
-                in_=tab_scales[:, 4 * q : 4 * q + 4, :].bitcast(I32),
-            )
-
-        def load_wk_scales(q, queue=nc.sync):
-            queue.dma_start(
-                out=wk_sc[32 * q : 32 * q + 4, :, :],
-                in_=wk_scales[:, 4 * q : 4 * q + 4, :].rearrange("a r n -> r a n").bitcast(I32),
-            )
 
         load_tab(0, 1)
         nc.sync.dma_start(offsets[:], offs)
         for q in range(QUADS):
-            load_tab_scales(q, nc.sync if q < QUADS // 2 else nc.scalar)
-        nc.scalar.activation(out=bias0[:], in_=zero[:], func=SILU)
-        load_tab(1, 2)
-        load_wk(0, 3)
+            queue = nc.sync if q < QUADS // 2 else nc.scalar
+            queue.dma_start(
+                out=tab_sc[32 * q : 32 * q + SCALE_ROWS * PASSES, :],
+                in_=tab_scales[:, SCALE_ROWS * q : SCALE_ROWS * (q + 1), :].bitcast(I32),
+            )
+        nc.scalar.activation(out=silu_bias[:], in_=zero[:], func=SILU)
+        load_tab(1, PASSES)
+        nc.sync.dma_start(out=wk[:], in_=wk_words.rearrange("a p n i -> p a (n i)").bitcast(I32))
         for q in range(QUADS):
-            load_wk_scales(q)
-        load_tab(2, 3)
-        load_wv(0, 1)
-        load_wv(1, 2)
-        load_wv(2, 3)
-        load_half("st", st_sb, st, 0, 0)
-        load_half("st", st_sb, st, 0, 1)
-        load_half("res", res_sb, res, 0, 0)
+            nc.sync.dma_start(
+                out=wk_sc[32 * q : 32 * q + SCALE_ROWS, :, :],
+                in_=wk_scales[:, SCALE_ROWS * q : SCALE_ROWS * (q + 1), :].rearrange("a r n -> r a n").bitcast(I32),
+            )
+        for a in range(PASSES):
+            load_wv(a)
+        st_sb[0] = sb("st0", [P, J], F32)[:]
+        for c in range(HALVES):
+            nc.sync.dma_start(out=st_sb[0][:, jcols(c)], in_=st[0:P, jcols(c)])
+        load_rows("res", res_sb, res, 0, 1)
         load_rows("st", st_sb, st, 1, 2)
-        load_half("res", res_sb, res, 0, 1)
         load_rows("st", st_sb, st, 2, 3)
         load_rows("res", res_sb, res, 1, 2)
         load_rows("st", st_sb, st, 3, 4)
-        load_rows("res", res_sb, res, 2, 3)
-        load_rows("res", res_sb, res, 3, 4)
+        load_rows("res", res_sb, res, 2, 4)
 
         def gather_words(a):
             nc.vector.tensor_copy(out=got[a][:], in_=tab[a].bitcast(U32).indirect(offsets[:]))
 
-        def cast(copy, a, n0, n1):
+        def round_wv(copy, a, n0, n1):
             copy(
                 out=wv_bf[a][:, n0:n1, :].rearrange("p (c u) i -> p c i u", u=4),
                 in_=wv_raw[a][:, :, n0:n1].rearrange("p i (c u) -> p c i u", u=4),
@@ -136,14 +125,8 @@ def tile_list_engram_silu_kernel(tc, tab_words, tab_scales, wk_words, wk_scales,
                 in_=wv_bf[a][:, n0:n1, :].rearrange("p n i -> p (n i)"),
             )
 
-        def ncols(c):
-            return slice((c // HALVES) * P, (c // HALVES + 1) * P)
-
-        def jcols(c):
-            return slice((c % HALVES) * BANK, (c % HALVES + 1) * BANK)
-
         free_banks = list(range(BANKS))
-        bank_of, acc, gate, prod = {}, {}, {}, {}
+        bank_of, acc, gate, prod, whole = {}, {}, {}, {}, {}
 
         def mx_pass(kind, c, a):
             if a == 0:
@@ -158,52 +141,60 @@ def tile_list_engram_silu_kernel(tc, tab_words, tab_scales, wk_words, wk_scales,
                 lhsT=words.bitcast(FP8X4),
                 lhsT_scale=scales,
                 rhs=got[a][:, jcols(c)].bitcast(FP8X4),
-                rhs_scale=got_sc[4 * a : P, jcols(c)],
+                rhs_scale=got_sc[SCALE_ROWS * a : P, jcols(c)],
                 start=(a == 0),
-                stop=(a == PASSES - 1),
+                stop=(a == LAST),
             )
 
         def make_gate(c):
             s = sb(f"s{c}", [P, BANK], F32, tag="last" if c == CHUNKS - 1 else None)
             nc.vector.tensor_tensor(out=s[:], in0=acc["ke", c][:], in1=st_sb[c // HALVES][:, jcols(c)], op=MULT)
             gate[c] = sb(f"gate{c}", [P, BANK], F32)
-            nc.scalar.activation(out=gate[c][:], in_=s[:], func=SILU, bias=bias0[:])
+            nc.scalar.activation(out=gate[c][:], in_=s[:], func=SILU, bias=silu_bias[:])
 
         def gate_value(c):
             prod[c] = sb(f"prod{c}", [P, BANK], F32)
             nc.vector.tensor_tensor(out=prod[c][:], in0=acc["ve", c][:], in1=gate[c][:], op=MULT)
 
-        def finish(c):
+        def add_res(engine, c, dst):
+            engine.tensor_tensor(out=dst, in0=prod[c][:], in1=res_sb[c // HALVES][:, jcols(c)], op=ADD)
+
+        def pool_finish(c):
             n = c // HALVES
-            nc.gpsimd.tensor_tensor(out=out_sb[n][:, jcols(c)], in0=prod[c][:], in1=res_sb[n][:, jcols(c)], op=ADD)
             if n >= WHOLE_STORES:
-                nc.sync.dma_start(out=out[ncols(c), jcols(c)], in_=out_sb[n][:, jcols(c)])
-            elif c % HALVES == HALVES - 1:
-                nc.sync.dma_start(out=out[ncols(c), :], in_=out_sb[n][:])
+                part = sb(f"out_chunk{c}", [P, BANK], F32)
+                add_res(nc.gpsimd, c, part[:])
+                nc.sync.dma_start(out=out[ncols(c), jcols(c)], in_=part[:])
+                return
+            if c % HALVES == 0:
+                whole[n] = sb(f"out_rows{n}", [P, J], F32)
+            add_res(nc.gpsimd, c, whole[n][:, jcols(c)])
+            if c % HALVES == HALVES - 1:
+                nc.sync.dma_start(out=out[ncols(c), :], in_=whole[n][:])
 
         ke_first = range(KE_FIRST)
         ve_first = range(BANKS - KE_FIRST)
         gather_words(0)
         nc.vector.tensor_copy(out=got_sc[:], in_=tab_sc[:].bitcast(U8).indirect(offsets[:]))
-        gather_words(1)
-        gather_words(2)
+        for a in range(1, PASSES):
+            gather_words(a)
         for a in range(PASSES):
             for c in ke_first:
                 mx_pass("ke", c, a)
-        cast(nc.scalar.copy, 0, 0, N)
-        cast(nc.vector.tensor_copy, 1, 0, N // 2)
-        cast(nc.scalar.copy, 1, N // 2, N)
-        for a in range(PASSES - 1):
+        round_wv(nc.scalar.copy, 0, 0, N)
+        round_wv(nc.vector.tensor_copy, 1, 0, N // 2)
+        round_wv(nc.scalar.copy, 1, N // 2, N)
+        for a in range(LAST):
             quantize(a, 0, N)
-        for a in range(PASSES - 1):
+        for a in range(LAST):
             for c in ve_first:
                 mx_pass("ve", c, a)
-        cast(nc.vector.tensor_copy, 2, 0, P)
-        cast(nc.scalar.copy, 2, P, 2 * P)
-        cast(nc.scalar.copy, 2, 2 * P, N)
-        quantize(2, 0, N // 2)
+        round_wv(nc.vector.tensor_copy, LAST, 0, P)
+        round_wv(nc.scalar.copy, LAST, P, 2 * P)
+        round_wv(nc.scalar.copy, LAST, 2 * P, N)
+        quantize(LAST, 0, N // 2)
         for c in ve_first:
-            mx_pass("ve", c, 2)
+            mx_pass("ve", c, LAST)
 
         steps = [("ke", 0)]
         for c in range(CHUNKS):
@@ -217,17 +208,18 @@ def tile_list_engram_silu_kernel(tc, tab_words, tab_scales, wk_words, wk_scales,
                 make_gate(c)
             else:
                 if c == 0:
-                    quantize(2, N // 2, N)
+                    quantize(LAST, N // 2, N)
                 gate_value(c)
             free_banks.append(bank_of[kind, c])
             if later:
-                step = later.pop(0)
+                next_kind, next_c = later.pop(0)
                 for a in range(PASSES):
-                    mx_pass(step[0], step[1], a)
+                    mx_pass(next_kind, next_c, a)
             if kind == "ve" and c < POOL_CHUNKS:
-                finish(c)
+                pool_finish(c)
+
         late = sb("late", [P, CHUNKS - POOL_CHUNKS, BANK], F32, tag="last")
         for c in range(POOL_CHUNKS, CHUNKS):
             dst = late[:, c - POOL_CHUNKS, :]
-            nc.vector.tensor_tensor(out=dst, in0=prod[c][:], in1=res_sb[c // HALVES][:, jcols(c)], op=ADD)
+            add_res(nc.vector, c, dst)
             nc.sync.dma_start(out=out[ncols(c), jcols(c)], in_=dst)

@@ -28,7 +28,8 @@ HALVES = J // BANK
 NT = N // P
 CHUNKS = NT * HALVES
 POOL_CHUNKS = 5
-KE_FIRST = 6
+KE_FIRST = 4
+HALF = N // 2
 WHOLE_STORES = 2
 
 
@@ -49,7 +50,7 @@ def tile_list_engram_silu_kernel(tc, tab_words, tab_scales, wk_words, wk_scales,
 
         offsets = sb("offsets", [P, J // 16], U16)
         tab_sc = sb("tab_sc", [P, T // 4], I32)
-        wk = sb("wk", [P, PASSES, N], I32)
+        wk = [sb(f"wk{h}", [P, PASSES, HALF], I32) for h in range(2)]
         wk_sc = sb("wk_sc", [P, PASSES, N // 4], I32)
         wv_bf = [sb(f"wv_bf{a}", [P, N, PACK], BF16) for a in range(PASSES)]
         wv_q = [sb(f"wv_q{a}", [P, N], U32) for a in range(PASSES)]
@@ -69,6 +70,10 @@ def tile_list_engram_silu_kernel(tc, tab_words, tab_scales, wk_words, wk_scales,
             nc.sync.dma_start(out=tile[:], in_=tab_words[a0:a1].rearrange("a p t i -> p a (t i)").bitcast(I32))
             for a in range(a0, a1):
                 tab[a] = tile[:, a - a0, :]
+
+        def load_wk(h):
+            cols = wk_words[:, :, h * HALF : (h + 1) * HALF, :]
+            nc.sync.dma_start(out=wk[h][:], in_=cols.rearrange("a p n i -> p a (n i)").bitcast(I32))
 
         def load_wv(a):
             wv_raw[a] = sb(f"wv_raw{a}", [P, PACK, N], F32)
@@ -91,7 +96,7 @@ def tile_list_engram_silu_kernel(tc, tab_words, tab_scales, wk_words, wk_scales,
             )
         nc.scalar.activation(out=silu_bias[:], in_=zero[:], func=SILU)
         load_tab(1, PASSES)
-        nc.sync.dma_start(out=wk[:], in_=wk_words.rearrange("a p n i -> p a (n i)").bitcast(I32))
+        load_wk(0)
         for q in range(QUADS):
             nc.sync.dma_start(
                 out=wk_sc[32 * q : 32 * q + SCALE_ROWS, :, :],
@@ -99,15 +104,15 @@ def tile_list_engram_silu_kernel(tc, tab_words, tab_scales, wk_words, wk_scales,
             )
         for a in range(PASSES):
             load_wv(a)
-        st_sb[0] = sb("st0", [P, J], F32)[:]
-        for c in range(HALVES):
-            nc.sync.dma_start(out=st_sb[0][:, jcols(c)], in_=st[0:P, jcols(c)])
-        load_rows("res", res_sb, res, 0, 1)
+        load_rows("st", st_sb, st, 0, 1)
         load_rows("st", st_sb, st, 1, 2)
+        load_wk(1)
+        load_rows("res", res_sb, res, 0, 1)
         load_rows("st", st_sb, st, 2, 3)
         load_rows("res", res_sb, res, 1, 2)
         load_rows("st", st_sb, st, 3, 4)
-        load_rows("res", res_sb, res, 2, 4)
+        load_rows("res", res_sb, res, 2, 3)
+        load_rows("res", res_sb, res, 3, 4)
 
         def gather_words(a):
             nc.vector.tensor_copy(out=got[a][:], in_=tab[a].bitcast(U32).indirect(offsets[:]))
@@ -133,7 +138,8 @@ def tile_list_engram_silu_kernel(tc, tab_words, tab_scales, wk_words, wk_scales,
                 bank_of[kind, c] = free_banks.pop(0)
                 acc[kind, c] = psum.tile([P, BANK], F32, name=f"bank{bank_of[kind, c]}")
             if kind == "ke":
-                words, scales = wk[:, a, ncols(c)], wk_sc[:].bitcast(U8)[:, a, ncols(c)]
+                h, t = divmod(c // HALVES, 2)
+                words, scales = wk[h][:, a, t * P : (t + 1) * P], wk_sc[:].bitcast(U8)[:, a, ncols(c)]
             else:
                 words, scales = wv_q[a][:, ncols(c)], wv_sc[a][:, ncols(c)]
             nc.tensor.matmul_mx(
@@ -153,11 +159,14 @@ def tile_list_engram_silu_kernel(tc, tab_words, tab_scales, wk_words, wk_scales,
             nc.scalar.activation(out=gate[c][:], in_=s[:], func=SILU, bias=silu_bias[:])
 
         def gate_value(c):
-            prod[c] = sb(f"prod{c}", [P, BANK], F32)
-            nc.vector.tensor_tensor(out=prod[c][:], in0=acc["ve", c][:], in1=gate[c][:], op=MULT)
+            if c % HALVES == HALVES - 1 and c + 1 < CHUNKS:
+                prod[c] = st_sb[(c + 1) // HALVES][:, jcols(c + 1)]
+            else:
+                prod[c] = sb(f"prod{c}", [P, BANK], F32)[:]
+            nc.vector.tensor_tensor(out=prod[c], in0=acc["ve", c][:], in1=gate[c][:], op=MULT)
 
         def add_res(engine, c, dst):
-            engine.tensor_tensor(out=dst, in0=prod[c][:], in1=res_sb[c // HALVES][:, jcols(c)], op=ADD)
+            engine.tensor_tensor(out=dst, in0=prod[c], in1=res_sb[c // HALVES][:, jcols(c)], op=ADD)
 
         def pool_finish(c):
             n = c // HALVES
@@ -181,7 +190,8 @@ def tile_list_engram_silu_kernel(tc, tab_words, tab_scales, wk_words, wk_scales,
         for a in range(PASSES):
             for c in ke_first:
                 mx_pass("ke", c, a)
-        round_wv(nc.scalar.copy, 0, 0, N)
+        round_wv(nc.scalar.copy, 0, 0, N // 2)
+        round_wv(nc.vector.tensor_copy, 0, N // 2, N)
         round_wv(nc.vector.tensor_copy, 1, 0, N // 2)
         round_wv(nc.scalar.copy, 1, N // 2, N)
         for a in range(LAST):
@@ -196,19 +206,21 @@ def tile_list_engram_silu_kernel(tc, tab_words, tab_scales, wk_words, wk_scales,
         for c in ve_first:
             mx_pass("ve", c, LAST)
 
-        steps = [("ke", 0)]
-        for c in range(CHUNKS):
-            if c + 1 < CHUNKS:
-                steps.append(("ke", c + 1))
-            steps.append(("ve", c))
+        steps = []
+        for n in range(NT):
+            steps.extend(("ke", c) for c in range(HALVES * n, HALVES * (n + 1)))
+            steps.extend(("ve", c) for c in range(max(HALVES * n - 1, 0), HALVES * n + 1))
+        steps.append(("ve", CHUNKS - 1))
         later = [step for step in steps if step not in bank_of]
+        later.remove(("ve", KE_FIRST))
+        later.insert(0, ("ve", KE_FIRST))
 
         for kind, c in steps:
             if kind == "ke":
                 make_gate(c)
-            else:
                 if c == 0:
                     quantize(LAST, N // 2, N)
+            else:
                 gate_value(c)
             free_banks.append(bank_of[kind, c])
             if later:

@@ -106,8 +106,8 @@ def tile_list_engram_silu_kernel(tc, tab_words, tab_scales, wk_words, wk_scales,
             load_wv(a)
         load_rows("st", st_sb, st, 0, 1)
         load_rows("st", st_sb, st, 1, 2)
-        load_wk(1)
         load_rows("res", res_sb, res, 0, 1)
+        load_wk(1)
         load_rows("st", st_sb, st, 2, 3)
         load_rows("res", res_sb, res, 1, 2)
         load_rows("st", st_sb, st, 3, 4)
@@ -212,8 +212,9 @@ def tile_list_engram_silu_kernel(tc, tab_words, tab_scales, wk_words, wk_scales,
             steps.extend(("ve", c) for c in range(max(HALVES * n - 1, 0), HALVES * n + 1))
         steps.append(("ve", CHUNKS - 1))
         later = [step for step in steps if step not in bank_of]
-        later.remove(("ve", KE_FIRST))
-        later.insert(0, ("ve", KE_FIRST))
+        for c in reversed(range(KE_FIRST, KE_FIRST + HALVES)):
+            later.remove(("ve", c))
+            later.insert(0, ("ve", c))
 
         for kind, c in steps:
             if kind == "ke":

@@ -40,7 +40,7 @@ def tile_list_engram_silu_kernel(tc, tab_words, tab_scales, wk_words, wk_scales,
         psum = ctx.enter_context(tc.psum_pool(name="psum", bufs=1))
 
         def sb(name, shape, dtype, tag=None):
-            return keep.tile(shape, dtype, name=name, tag=tag or name, align_bytes=64)
+            return keep.tile(shape, dtype, name=name, tag=tag or name, align_bytes=256)
 
         def ncols(c):
             return slice((c // HALVES) * P, (c // HALVES + 1) * P)

@@ -201,7 +201,8 @@ def tile_list_engram_silu_kernel(tc, tab_words, tab_scales, wk_words, wk_scales,
                 mx_pass("ve", c, a)
         round_wv(nc.vector.tensor_copy, LAST, 0, P)
         round_wv(nc.scalar.copy, LAST, P, 2 * P)
-        round_wv(nc.scalar.copy, LAST, 2 * P, N)
+        round_wv(nc.vector.tensor_copy, LAST, 2 * P, 3 * P)
+        round_wv(nc.scalar.copy, LAST, 3 * P, N)
         quantize(LAST, 0, N // 2)
         for c in ve_first:
             mx_pass("ve", c, LAST)

@@ -28,6 +28,8 @@ HALVES = J // BANK
 NT = N // P
 CHUNKS = NT * HALVES
 POOL_CHUNKS = 5
+POOL_COLS = 256
+POOL_GATE = 3
 KE_FIRST = 4
 HALF = N // 2
 WHOLE_STORES = 2
@@ -158,6 +160,17 @@ def tile_list_engram_silu_kernel(tc, tab_words, tab_scales, wk_words, wk_scales,
             gate[c] = sb(f"gate{c}", [P, BANK], F32)
             nc.scalar.activation(out=gate[c][:], in_=s[:], func=SILU, bias=silu_bias[:])
 
+        def pool_gate(c):
+            ke = wv_raw[LAST][:, :, N - P : N]
+            nc.scalar.copy(out=ke, in_=acc["ke", c][:].rearrange("p (i n) -> p i n", i=PACK))
+            s = wv_bf[LAST][:, N // 2 : N, :].rearrange("p n i -> p (n i)").bitcast(F32)
+            rows = st_sb[c // HALVES][:, jcols(c)]
+            nc.gpsimd.tensor_tensor(
+                out=s.rearrange("p (i n) -> p i n", i=PACK), in0=ke, in1=rows.rearrange("p (i n) -> p i n", i=PACK), op=MULT
+            )
+            gate[c] = sb(f"gate{c}", [P, BANK], F32)
+            nc.scalar.activation(out=gate[c][:], in_=s, func=SILU, bias=silu_bias[:])
+
         def gate_value(c):
             if c % HALVES == HALVES - 1 and c + 1 < CHUNKS:
                 prod[c] = st_sb[(c + 1) // HALVES][:, jcols(c + 1)]
@@ -165,8 +178,9 @@ def tile_list_engram_silu_kernel(tc, tab_words, tab_scales, wk_words, wk_scales,
                 prod[c] = sb(f"prod{c}", [P, BANK], F32)[:]
             nc.vector.tensor_tensor(out=prod[c], in0=acc["ve", c][:], in1=gate[c][:], op=MULT)
 
-        def add_res(engine, c, dst):
-            engine.tensor_tensor(out=dst, in0=prod[c], in1=res_sb[c // HALVES][:, jcols(c)], op=ADD)
+        def add_res(engine, c, dst, cols=slice(0, BANK)):
+            rows = res_sb[c // HALVES][:, jcols(c)]
+            engine.tensor_tensor(out=dst[:, cols], in0=prod[c][:, cols], in1=rows[:, cols], op=ADD)
 
         def pool_finish(c):
             n = c // HALVES
@@ -212,13 +226,17 @@ def tile_list_engram_silu_kernel(tc, tab_words, tab_scales, wk_words, wk_scales,
             steps.extend(("ke", c) for c in range(HALVES * n, HALVES * (n + 1)))
             steps.extend(("ve", c) for c in range(max(HALVES * n - 1, 0), HALVES * n + 1))
         steps.append(("ve", CHUNKS - 1))
+        steps.remove(("ke", POOL_GATE))
+        steps.insert(1, ("ke", POOL_GATE))
         later = [step for step in steps if step not in bank_of]
         for c in reversed(range(KE_FIRST, KE_FIRST + HALVES)):
             later.remove(("ve", c))
             later.insert(0, ("ve", c))
 
         for kind, c in steps:
-            if kind == "ke":
+            if (kind, c) == ("ke", POOL_GATE):
+                pool_gate(c)
+            elif kind == "ke":
                 make_gate(c)
                 if c == 0:
                     quantize(LAST, N // 2, N)
@@ -235,5 +253,9 @@ def tile_list_engram_silu_kernel(tc, tab_words, tab_scales, wk_words, wk_scales,
         late = sb("late", [P, CHUNKS - POOL_CHUNKS, BANK], F32, tag="last")
         for c in range(POOL_CHUNKS, CHUNKS):
             dst = late[:, c - POOL_CHUNKS, :]
-            add_res(nc.vector, c, dst)
+            if c == POOL_CHUNKS:
+                add_res(nc.gpsimd, c, dst, slice(0, POOL_COLS))
+                add_res(nc.vector, c, dst, slice(POOL_COLS, BANK))
+            else:
+                add_res(nc.vector, c, dst)
             nc.sync.dma_start(out=out[ncols(c), jcols(c)], in_=dst)

@@ -28,8 +28,8 @@ HALVES = J // BANK
 NT = N // P
 CHUNKS = NT * HALVES
 POOL_CHUNKS = 5
-POOL_COLS = 256
 POOL_GATE = 3
+WIDE_TILE = 1
 KE_FIRST = 4
 HALF = N // 2
 WHOLE_STORES = 2
@@ -61,6 +61,7 @@ def tile_list_engram_silu_kernel(tc, tab_words, tab_scales, wk_words, wk_scales,
         got_sc = sb("got_sc", [P, J], U8)
         zero = sb("zero", [P, 1], F32)
         silu_bias = sb("silu_bias", [P, 1], F32)
+        wide = sb("wide", [P, J], F32)
         tab, wv_raw, st_sb, res_sb = {}, {}, {}, {}
 
         nc.vector.memset(tab_sc[:], 0)
@@ -172,15 +173,16 @@ def tile_list_engram_silu_kernel(tc, tab_words, tab_scales, wk_words, wk_scales,
             nc.scalar.activation(out=gate[c][:], in_=s, func=SILU, bias=silu_bias[:])
 
         def gate_value(c):
-            if c % HALVES == HALVES - 1 and c + 1 < CHUNKS:
+            if c // HALVES == WIDE_TILE:
+                prod[c] = wide[:, jcols(c)]
+            elif c % HALVES == HALVES - 1 and c + 1 < CHUNKS:
                 prod[c] = st_sb[(c + 1) // HALVES][:, jcols(c + 1)]
             else:
                 prod[c] = sb(f"prod{c}", [P, BANK], F32)[:]
             nc.vector.tensor_tensor(out=prod[c], in0=acc["ve", c][:], in1=gate[c][:], op=MULT)
 
-        def add_res(engine, c, dst, cols=slice(0, BANK)):
-            rows = res_sb[c // HALVES][:, jcols(c)]
-            engine.tensor_tensor(out=dst[:, cols], in0=prod[c][:, cols], in1=rows[:, cols], op=ADD)
+        def add_res(engine, c, dst):
+            engine.tensor_tensor(out=dst, in0=prod[c], in1=res_sb[c // HALVES][:, jcols(c)], op=ADD)
 
         def pool_finish(c):
             n = c // HALVES
@@ -188,6 +190,11 @@ def tile_list_engram_silu_kernel(tc, tab_words, tab_scales, wk_words, wk_scales,
                 part = sb(f"out_chunk{c}", [P, BANK], F32)
                 add_res(nc.gpsimd, c, part[:])
                 nc.sync.dma_start(out=out[ncols(c), jcols(c)], in_=part[:])
+                return
+            if n == WIDE_TILE:
+                if c % HALVES == HALVES - 1:
+                    nc.gpsimd.tensor_tensor(out=wide[:], in0=wide[:], in1=res_sb[n], op=ADD)
+                    nc.sync.dma_start(out=out[ncols(c), :], in_=wide[:])
                 return
             if c % HALVES == 0:
                 whole[n] = sb(f"out_rows{n}", [P, J], F32)
@@ -228,6 +235,8 @@ def tile_list_engram_silu_kernel(tc, tab_words, tab_scales, wk_words, wk_scales,
         steps.append(("ve", CHUNKS - 1))
         steps.remove(("ke", POOL_GATE))
         steps.insert(1, ("ke", POOL_GATE))
+        steps.remove(("ve", POOL_GATE))
+        steps.insert(steps.index(("ve", POOL_GATE - 1)) + 1, ("ve", POOL_GATE))
         later = [step for step in steps if step not in bank_of]
         for c in reversed(range(KE_FIRST, KE_FIRST + HALVES)):
             later.remove(("ve", c))
@@ -253,9 +262,5 @@ def tile_list_engram_silu_kernel(tc, tab_words, tab_scales, wk_words, wk_scales,
         late = sb("late", [P, CHUNKS - POOL_CHUNKS, BANK], F32, tag="last")
         for c in range(POOL_CHUNKS, CHUNKS):
             dst = late[:, c - POOL_CHUNKS, :]
-            if c == POOL_CHUNKS:
-                add_res(nc.gpsimd, c, dst, slice(0, POOL_COLS))
-                add_res(nc.vector, c, dst, slice(POOL_COLS, BANK))
-            else:
-                add_res(nc.vector, c, dst)
+            add_res(nc.vector, c, dst)
             nc.sync.dma_start(out=out[ncols(c), jcols(c)], in_=dst)

@@ -162,8 +162,7 @@ def tile_list_engram_silu_kernel(tc, tab_words, tab_scales, wk_words, wk_scales,
             nc.scalar.activation(out=gate[c][:], in_=s[:], func=SILU, bias=silu_bias[:])
 
         def pool_gate(c):
-            ke = wv_raw[LAST][:, :, N - P : N]
-            nc.scalar.copy(out=ke, in_=acc["ke", c][:].rearrange("p (i n) -> p i n", i=PACK))
+            ke = wv_raw[LAST - 1][:, :, N - P : N]
             s = wv_bf[LAST][:, N // 2 : N, :].rearrange("p n i -> p (n i)").bitcast(F32)
             rows = st_sb[c // HALVES][:, jcols(c)]
             nc.gpsimd.tensor_tensor(
@@ -220,6 +219,10 @@ def tile_list_engram_silu_kernel(tc, tab_words, tab_scales, wk_words, wk_scales,
         for a in range(LAST):
             for c in ve_first:
                 mx_pass("ve", c, a)
+        nc.scalar.copy(out=wv_raw[LAST - 1][:, :, N - P : N], in_=acc["ke", POOL_GATE][:].rearrange("p (i n) -> p i n", i=PACK))
+        free_banks.append(bank_of["ke", POOL_GATE])
+        for a in range(LAST):
+            mx_pass("ve", KE_FIRST, a)
         round_wv(nc.vector.tensor_copy, LAST, 0, P)
         round_wv(nc.scalar.copy, LAST, P, 2 * P)
         round_wv(nc.vector.tensor_copy, LAST, 2 * P, 3 * P)
@@ -234,21 +237,19 @@ def tile_list_engram_silu_kernel(tc, tab_words, tab_scales, wk_words, wk_scales,
             steps.extend(("ve", c) for c in range(max(HALVES * n - 1, 0), HALVES * n + 1))
         steps.append(("ve", CHUNKS - 1))
         steps.remove(("ke", POOL_GATE))
-        steps.insert(1, ("ke", POOL_GATE))
         steps.remove(("ve", POOL_GATE))
         steps.insert(steps.index(("ve", POOL_GATE - 1)) + 1, ("ve", POOL_GATE))
         later = [step for step in steps if step not in bank_of]
-        for c in reversed(range(KE_FIRST, KE_FIRST + HALVES)):
-            later.remove(("ve", c))
-            later.insert(0, ("ve", c))
+        later.remove(("ve", KE_FIRST + 1))
+        later.insert(0, ("ve", KE_FIRST + 1))
 
         for kind, c in steps:
-            if (kind, c) == ("ke", POOL_GATE):
-                pool_gate(c)
-            elif kind == "ke":
+            if kind == "ke":
                 make_gate(c)
                 if c == 0:
                     quantize(LAST, N // 2, N)
+                    mx_pass("ve", KE_FIRST, LAST)
+                    pool_gate(POOL_GATE)
             else:
                 gate_value(c)
             free_banks.append(bank_of[kind, c])

@@ -98,13 +98,14 @@ def tile_list_engram_silu_kernel(tc, tab_words, tab_scales, wk_words, wk_scales,
                 in_=tab_scales[:, SCALE_ROWS * q : SCALE_ROWS * (q + 1), :].bitcast(I32),
             )
         nc.scalar.activation(out=silu_bias[:], in_=zero[:], func=SILU)
-        load_tab(1, PASSES)
+        load_tab(1, LAST)
         load_wk(0)
         for q in range(QUADS):
             nc.sync.dma_start(
                 out=wk_sc[32 * q : 32 * q + SCALE_ROWS, :, :],
                 in_=wk_scales[:, SCALE_ROWS * q : SCALE_ROWS * (q + 1), :].rearrange("a r n -> r a n").bitcast(I32),
             )
+        load_tab(LAST, PASSES)
         for a in range(PASSES):
             load_wv(a)
         load_rows("st", st_sb, st, 0, 1)

from contextlib import ExitStack

import concourse.mybir as mybir

K, N, T, J = 1536, 512, 2048, 1024
FLOPS = 2 * 2 * K * N * J

F32 = mybir.dt.float32
BF16 = mybir.dt.bfloat16
I32 = mybir.dt.int32
U32 = mybir.dt.uint32
U16 = mybir.dt.uint16
U8 = mybir.dt.uint8
FP8X4 = mybir.dt.float8_e4m3fn_x4
MULT = mybir.AluOpType.mult
ADD = mybir.AluOpType.add
SILU = mybir.ActivationFunctionType.Silu

P = 128
PACK = 4
PASSES = K // (P * PACK)
LAST = PASSES - 1
QUADS = 4
SCALE_ROWS = 4
BANK = 512
BANKS = 8
HALVES = J // BANK
NT = N // P
CHUNKS = NT * HALVES
POOL_CHUNKS = 5
POOL_GATE = 3
WIDE_TILE = 1
KE_FIRST = 4
HALF = N // 2
WHOLE_STORES = 2


def tile_list_engram_silu_kernel(tc, tab_words, tab_scales, wk_words, wk_scales, wv, st, res, offs, out):
    nc = tc.nc
    with ExitStack() as ctx:
        keep = ctx.enter_context(tc.tile_pool(name="keep", bufs=1))
        psum = ctx.enter_context(tc.psum_pool(name="psum", bufs=1))

        def sb(name, shape, dtype, tag=None):
            return keep.tile(shape, dtype, name=name, tag=tag or name, align_bytes=256)

        def ncols(c):
            return slice((c // HALVES) * P, (c // HALVES + 1) * P)

        def jcols(c):
            return slice((c % HALVES) * BANK, (c % HALVES + 1) * BANK)

        offsets = sb("offsets", [P, J // 16], U16)
        tab_sc = sb("tab_sc", [P, T // 4], I32)
        wk = [sb(f"wk{h}", [P, PASSES, HALF], I32) for h in range(2)]
        wk_sc = sb("wk_sc", [P, PASSES, N // 4], I32)
        wv_bf = [sb(f"wv_bf{a}", [P, N, PACK], BF16) for a in range(PASSES)]
        wv_q = [sb(f"wv_q{a}", [P, N], U32) for a in range(PASSES)]
        wv_sc = [sb(f"wv_sc{a}", [P, N], U8) for a in range(PASSES)]
        got = [sb(f"got{a}", [P, J], U32) for a in range(PASSES)]
        got_sc = sb("got_sc", [P, J], U8)
        zero = sb("zero", [P, 1], F32)
        silu_bias = sb("silu_bias", [P, 1], F32)
        wide = sb("wide", [P, J], F32)
        tab, wv_raw, st_sb, res_sb = {}, {}, {}, {}

        nc.vector.memset(tab_sc[:], 0)
        nc.vector.memset(wk_sc[:], 0)
        nc.vector.memset(zero[:], 0.0)

        def load_tab(a0, a1):
            tile = sb(f"tab{a0}", [P, a1 - a0, T], I32)
            nc.sync.dma_start(out=tile[:], in_=tab_words[a0:a1].rearrange("a p t i -> p a (t i)").bitcast(I32))
            for a in range(a0, a1):
                tab[a] = tile[:, a - a0, :]

        def load_wk(h):
            cols = wk_words[:, :, h * HALF : (h + 1) * HALF, :]
            nc.sync.dma_start(out=wk[h][:], in_=cols.rearrange("a p n i -> p a (n i)").bitcast(I32))

        def load_wv(a):
            wv_raw[a] = sb(f"wv_raw{a}", [P, PACK, N], F32)
            rows = wv[a * P * PACK : (a + 1) * P * PACK, :]
            nc.sync.dma_start(out=wv_raw[a][:], in_=rows.rearrange("(p i) n -> p i n", i=PACK))

        def load_rows(name, tiles, src, n0, n1):
            tile = sb(f"{name}{n0}", [P, n1 - n0, J], F32)
            nc.sync.dma_start(out=tile[:], in_=src[n0 * P : n1 * P, :].rearrange("(c p) j -> p c j", p=P))
            for n in range(n0, n1):
                tiles[n] = tile[:, n - n0, :]

        load_tab(0, 1)
        nc.sync.dma_start(offsets[:], offs)
        for q in range(QUADS):
            queue = nc.sync if q < QUADS // 2 else nc.scalar
            queue.dma_start(
                out=tab_sc[32 * q : 32 * q + SCALE_ROWS * PASSES, :],
                in_=tab_scales[:, SCALE_ROWS * q : SCALE_ROWS * (q + 1), :].bitcast(I32),
            )
        nc.scalar.activation(out=silu_bias[:], in_=zero[:], func=SILU)
        load_tab(1, LAST)
        load_wk(0)
        for q in range(QUADS):
            nc.sync.dma_start(
                out=wk_sc[32 * q : 32 * q + SCALE_ROWS, :, :],
                in_=wk_scales[:, SCALE_ROWS * q : SCALE_ROWS * (q + 1), :].rearrange("a r n -> r a n").bitcast(I32),
            )
        load_tab(LAST, PASSES)
        for a in range(PASSES):
            load_wv(a)
        load_rows("st", st_sb, st, 0, 1)
        load_rows("st", st_sb, st, 1, 2)
        load_rows("res", res_sb, res, 0, 1)
        load_wk(1)
        load_rows("st", st_sb, st, 2, 3)
        load_rows("res", res_sb, res, 1, 2)
        load_rows("st", st_sb, st, 3, 4)
        load_rows("res", res_sb, res, 2, 3)
        load_rows("res", res_sb, res, 3, 4)

        def gather_words(a):
            nc.vector.tensor_copy(out=got[a][:], in_=tab[a].bitcast(U32).indirect(offsets[:]))

        def round_wv(copy, a, n0, n1):
            copy(
                out=wv_bf[a][:, n0:n1, :].rearrange("p (c u) i -> p c i u", u=4),
                in_=wv_raw[a][:, :, n0:n1].rearrange("p i (c u) -> p c i u", u=4),
            )

        def quantize(a, n0, n1):
            nc.vector.quantize_mx(
                out=wv_q[a][:, n0:n1].bitcast(FP8X4),
                scales=wv_sc[a][:, n0:n1],
                in_=wv_bf[a][:, n0:n1, :].rearrange("p n i -> p (n i)"),
            )

        free_banks = list(range(BANKS))
        bank_of, acc, gate, prod, whole = {}, {}, {}, {}, {}

        def mx_pass(kind, c, a):
            if a == 0:
                bank_of[kind, c] = free_banks.pop(0)
                acc[kind, c] = psum.tile([P, BANK], F32, name=f"bank{bank_of[kind, c]}")
            if kind == "ke":
                h, t = divmod(c // HALVES, 2)
                words, scales = wk[h][:, a, t * P : (t + 1) * P], wk_sc[:].bitcast(U8)[:, a, ncols(c)]
            else:
                words, scales = wv_q[a][:, ncols(c)], wv_sc[a][:, ncols(c)]
            nc.tensor.matmul_mx(
                out=acc[kind, c][:],
                lhsT=words.bitcast(FP8X4),
                lhsT_scale=scales,
                rhs=got[a][:, jcols(c)].bitcast(FP8X4),
                rhs_scale=got_sc[SCALE_ROWS * a : P, jcols(c)],
                start=(a == 0),
                stop=(a == LAST),
            )

        def make_gate(c):
            s = sb(f"s{c}", [P, BANK], F32, tag="last" if c == CHUNKS - 1 else None)
            nc.vector.tensor_tensor(out=s[:], in0=acc["ke", c][:], in1=st_sb[c // HALVES][:, jcols(c)], op=MULT)
            gate[c] = sb(f"gate{c}", [P, BANK], F32)
            nc.scalar.activation(out=gate[c][:], in_=s[:], func=SILU, bias=silu_bias[:])

        def pool_gate(c):
            ke = wv_raw[LAST - 1][:, :, N - P : N]
            s = wv_bf[LAST][:, N // 2 : N, :].rearrange("p n i -> p (n i)").bitcast(F32)
            rows = st_sb[c // HALVES][:, jcols(c)]
            nc.gpsimd.tensor_tensor(
                out=s.rearrange("p (i n) -> p i n", i=PACK), in0=ke, in1=rows.rearrange("p (i n) -> p i n", i=PACK), op=MULT
            )
            gate[c] = sb(f"gate{c}", [P, BANK], F32)
            nc.scalar.activation(out=gate[c][:], in_=s, func=SILU, bias=silu_bias[:])

        def gate_value(c):
            if c // HALVES == WIDE_TILE:
                prod[c] = wide[:, jcols(c)]
            elif c % HALVES == HALVES - 1 and c + 1 < CHUNKS:
                prod[c] = st_sb[(c + 1) // HALVES][:, jcols(c + 1)]
            else:
                prod[c] = sb(f"prod{c}", [P, BANK], F32)[:]
            nc.vector.tensor_tensor(out=prod[c], in0=acc["ve", c][:], in1=gate[c][:], op=MULT)

        def add_res(engine, c, dst):
            engine.tensor_tensor(out=dst, in0=prod[c], in1=res_sb[c // HALVES][:, jcols(c)], op=ADD)

        def pool_finish(c):
            n = c // HALVES
            if n >= WHOLE_STORES:
                part = sb(f"out_chunk{c}", [P, BANK], F32)
                add_res(nc.gpsimd, c, part[:])
                nc.sync.dma_start(out=out[ncols(c), jcols(c)], in_=part[:])
                return
            if n == WIDE_TILE:
                if c % HALVES == HALVES - 1:
                    nc.gpsimd.tensor_tensor(out=wide[:], in0=wide[:], in1=res_sb[n], op=ADD)
                    nc.sync.dma_start(out=out[ncols(c), :], in_=wide[:])
                return
            if c % HALVES == 0:
                whole[n] = sb(f"out_rows{n}", [P, J], F32)
            add_res(nc.gpsimd, c, whole[n][:, jcols(c)])
            if c % HALVES == HALVES - 1:
                nc.sync.dma_start(out=out[ncols(c), :], in_=whole[n][:])

        ke_first = range(KE_FIRST)
        ve_first = range(BANKS - KE_FIRST)
        gather_words(0)
        nc.vector.tensor_copy(out=got_sc[:], in_=tab_sc[:].bitcast(U8).indirect(offsets[:]))
        for a in range(1, PASSES):
            gather_words(a)
        for a in range(PASSES):
            for c in ke_first:
                mx_pass("ke", c, a)
        round_wv(nc.scalar.copy, 0, 0, N // 2)
        round_wv(nc.vector.tensor_copy, 0, N // 2, N)
        round_wv(nc.vector.tensor_copy, 1, 0, N // 2)
        round_wv(nc.scalar.copy, 1, N // 2, N)
        for a in range(LAST):
            quantize(a, 0, N)
        for a in range(LAST):
            for c in ve_first:
                mx_pass("ve", c, a)
        nc.scalar.copy(out=wv_raw[LAST - 1][:, :, N - P : N], in_=acc["ke", POOL_GATE][:].rearrange("p (i n) -> p i n", i=PACK))
        free_banks.append(bank_of["ke", POOL_GATE])
        for a in range(LAST):
            mx_pass("ve", KE_FIRST, a)
        round_wv(nc.vector.tensor_copy, LAST, 0, P)
        round_wv(nc.scalar.copy, LAST, P, 2 * P)
        round_wv(nc.vector.tensor_copy, LAST, 2 * P, 3 * P)
        round_wv(nc.scalar.copy, LAST, 3 * P, N)
        quantize(LAST, 0, N // 2)
        for c in ve_first:
            mx_pass("ve", c, LAST)

        steps = []
        for n in range(NT):
            steps.extend(("ke", c) for c in range(HALVES * n, HALVES * (n + 1)))
            steps.extend(("ve", c) for c in range(max(HALVES * n - 1, 0), HALVES * n + 1))
        steps.append(("ve", CHUNKS - 1))
        steps.remove(("ke", POOL_GATE))
        steps.remove(("ve", POOL_GATE))
        steps.insert(steps.index(("ve", POOL_GATE - 1)) + 1, ("ve", POOL_GATE))
        later = [step for step in steps if step not in bank_of]
        later.remove(("ve", KE_FIRST + 1))
        later.insert(0, ("ve", KE_FIRST + 1))

        for kind, c in steps:
            if kind == "ke":
                make_gate(c)
                if c == 0:
                    quantize(LAST, N // 2, N)
                    mx_pass("ve", KE_FIRST, LAST)
                    pool_gate(POOL_GATE)
            else:
                gate_value(c)
            free_banks.append(bank_of[kind, c])
            if later:
                next_kind, next_c = later.pop(0)
                for a in range(PASSES):
                    mx_pass(next_kind, next_c, a)
            if kind == "ve" and c < POOL_CHUNKS:
                pool_finish(c)

        late = sb("late", [P, CHUNKS - POOL_CHUNKS, BANK], F32, tag="last")
        for c in range(POOL_CHUNKS, CHUNKS):
            dst = late[:, c - POOL_CHUNKS, :]
            add_res(nc.vector, c, dst)
            nc.sync.dma_start(out=out[ncols(c), jcols(c)], in_=dst)
